import numpy as np
import ml_dtypes


def mxq(x, axis, fmt="e4m3"):
    dtype, down = {"e4m3": (ml_dtypes.float8_e4m3fn, 7), "e5m2": (ml_dtypes.float8_e5m2, 14)}[fmt]
    v = np.moveaxis(np.asarray(x, np.float32).astype(ml_dtypes.bfloat16).astype(np.float64), axis, -1)
    blocks = v.reshape(v.shape[:-1] + (-1, 32))
    amax = np.abs(blocks).max(-1, keepdims=True)
    byte = np.maximum(np.where(amax > 0, np.frexp(amax)[1] - 1 + 127, 0) - down, 1)
    scale = np.exp2(byte - 127.0)
    codes = (blocks / scale).astype(np.float32).astype(dtype).astype(np.float64)
    return np.moveaxis((codes * scale).reshape(v.shape), -1, axis)


WIDE = False


def mx_kscale(k):
    if not WIDE:
        return np.ones(k)
    levels = np.array([10, -10, 5, -5, 0])
    if k % 512:
        return np.exp2(np.random.permutation(np.resize(levels, k // 32))).repeat(32)
    a = np.empty((k // 512, 16))
    for p in range(k // 512):
        a[p, :8] = np.random.permutation(np.resize(levels, 8))
        for g in range(8):
            far = levels[np.abs(levels - a[p, g]) >= 10]
            a[p, g + 8] = far[np.random.randint(len(far))]
    return np.exp2(a.ravel()).repeat(32)


def f64(x):
    return np.asarray(x).astype(np.float64)


def striped(idx):
    return np.tile(np.asarray(idx).reshape(-1, 16).T, (8, 1)).astype(np.uint16)


def unstriped(offs):
    return offs[:16].T.reshape(-1).astype(np.int64)


def striped8(idx):
    return np.asarray(idx).reshape(8, -1, 16).transpose(0, 2, 1).reshape(128, -1).astype(np.uint16)


def unstriped8(offs):
    return offs.reshape(8, 16, -1).transpose(0, 2, 1).reshape(8, -1).astype(np.int64)


def pick8(x, idx, run):
    r = np.arange(len(x))
    return x[r[:, None], idx[r % (8 * run) // run]]


E2M1 = np.array([0.0, 0.5, 1.0, 1.5, 2.0, 3.0, 4.0, 6.0, -0.0, -0.5, -1.0, -1.5, -2.0, -3.0, -4.0, -6.0])


def pack_weight(w, fmt):
    k, n = w.shape
    w = f64(np.asarray(w, np.float32).astype(ml_dtypes.bfloat16)).reshape(k // 32, 32, n)
    amax = np.abs(w).max(1)
    if fmt == "e4m3":
        byte = np.frexp(amax)[1] - 1 + 127 - 7
    else:
        mant, ex = np.frexp(amax / 6.0)
        byte = np.where(mant > 0.5, ex, ex - 1) + 127
    byte = np.clip(np.where(amax > 0, byte, 1), 1, 254)
    scaled = (w * np.exp2(127.0 - byte)[:, None, :]).reshape(k, n).astype(np.float32)
    by_word = np.ascontiguousarray(scaled.reshape(k // 512, 128, 4, n).transpose(0, 1, 3, 2))
    if fmt == "e4m3":
        words = by_word.astype(ml_dtypes.float8_e4m3fn).view(np.uint8)
    else:
        c = by_word.astype(ml_dtypes.float4_e2m1fn).view(np.uint8) & 0xF
        words = (c[..., 0::2] | (c[..., 1::2] << 4)).reshape(k // 512, 128, 2 * n)
    return np.ascontiguousarray(words), np.ascontiguousarray(byte.astype(np.uint8).reshape(k // 512, 16, n))


def unpack_weight(words, scales, fmt):
    g, _, n = scales.shape
    words = np.ascontiguousarray(words).reshape(g, 128, n, -1)
    if fmt == "e4m3":
        vals = words.view(ml_dtypes.float8_e4m3fn).astype(np.float64)
    else:
        nib = np.empty((g, 128, n, 4), np.uint8)
        nib[..., 0::2] = words & 0xF
        nib[..., 1::2] = words >> 4
        vals = E2M1[nib]
    vals = vals * np.repeat(np.exp2(scales.astype(np.float64) - 127.0), 8, axis=1)[..., None]
    return vals.transpose(0, 1, 3, 2).reshape(g * 512, n)


K, R, F, T, J, M, G = 512, 128, 512, 2048, 512, 256, 32


def setup_inputs():
    n = np.random.standard_normal
    idx = np.random.permutation(T)[:J]
    idx2 = np.stack([np.random.permutation(J)[:M] for _ in range(8)])
    fk = mx_kscale(K)
    dtabp = pack_weight(n((K, T)) / fk[:, None], "e2m1")
    tabp = pack_weight(n((K, T)) / fk[:, None], "e2m1")
    return {
        "dtab_words": dtabp[0],
        "dtab_scales": dtabp[1],
        "tab_words": tabp[0],
        "tab_scales": tabp[1],
        "w1": (n((K, R)) * 1 / np.sqrt(K) * fk[:, None]).astype(np.float32),
        "temper": (np.random.uniform(0.5, 1.5, (R, 1))).astype(np.float32),
        "pw": (np.random.uniform(0.5, 1.5, (1, M))).astype(np.float32),
        "og": (np.random.uniform(0.5, 2.0, (R, 1))).astype(np.float32),
        "base": (0.3 * n((R, M))).astype(np.float32),
        "offs": striped(idx),
        "offs2": striped8(idx2),
    }


def reference(dtab_words, dtab_scales, tab_words, tab_scales, w1, temper, pw, og, base, offs, offs2):
    idx = unstriped(offs)
    idx2 = unstriped8(offs2)
    dtabu = unpack_weight(dtab_words, dtab_scales, "e2m1")
    tabu = unpack_weight(tab_words, tab_scales, "e2m1")
    w1q = mxq(f64(w1), 0, "e4m3")
    tabidxg = tabu[:, idx]
    a = w1q.T @ tabidxg
    dtabidxg = dtabu[:, idx]
    ta = w1q.T @ dtabidxg
    p1 = np.exp(a * f64(temper))
    s = pick8(p1, idx2, 16) * f64(pw)
    z1 = s.reshape(R, G, M // G).sum(axis=2)
    zr = np.repeat(z1, M // G, axis=1)
    xp1 = ta * f64(temper) * p1
    xs = pick8(xp1, idx2, 16) * f64(pw)
    xz1 = xs.reshape(R, G, M // G).sum(axis=2)
    xzr = np.repeat(xz1, M // G, axis=1)
    xu1 = (xs - xzr * s / zr) / zr * 8.0 / (s / zr * 8.0 + 1.0)
    y = xu1 * f64(og) + f64(base)
    return y

from contextlib import ExitStack

import concourse.mybir as mybir
from concourse.masks import make_identity

K, R, T, J, M, G = 512, 128, 2048, 512, 256, 32
P = 128
GS = M // G
HALF = J // 2
FLOPS = 2 * 2 * K * R * J

F32 = mybir.dt.float32
BF16 = mybir.dt.bfloat16
I32 = mybir.dt.int32
U32 = mybir.dt.uint32
U16 = mybir.dt.uint16
U8 = mybir.dt.uint8
FP8X4 = mybir.dt.float8_e4m3fn_x4
FP4X4 = mybir.dt.float4_e2m1fn_x4
ALU = mybir.AluOpType
ACT = mybir.ActivationFunctionType
AX = mybir.AxisListType


def tile_attend_tcpickshares_kernel(tc, dtab_words, dtab_scales, tab_words, tab_scales, w1, temper, pw, og, base, offs, offs2, out):
    nc = tc.nc
    with ExitStack() as ctx:
        sb = ctx.enter_context(tc.tile_pool(name="sb", bufs=1))
        ps = ctx.enter_context(tc.psum_pool(name="ps", bufs=1))

        def t(name, cols, dtype, tag=None):
            return sb.tile([P, cols], dtype, name=name, tag=tag or name, align_bytes=64)

        slots = t("slots", J // 16, U16)
        picks = t("picks", M // 16, U16)
        tw = t("tw", T, U16)
        ts = t("ts", T, U8)
        ds = t("ds", T, U8)
        w_raw = t("w_raw", 4 * R, F32)
        temp = t("temp", 1, F32)
        gain = t("gain", 1, F32)
        weight = t("weight", M, F32)
        pw_cols = t("pw_cols", 2, F32)
        ident = t("ident", P, F32)

        def load_scales(tile, scales):
            for r in range(4):
                nc.sync.dma_start(tile[r:P:32, :].bitcast(I32), scales[0, r:16:4, :].bitcast(I32))

        nc.vector.memset(ts[:].bitcast(I32), 0)
        nc.vector.memset(ds[:].bitcast(I32), 0)
        nc.gpsimd.dma_start(pw_cols[:], pw.rearrange("o (p c) -> (o p) c", c=2))
        nc.gpsimd.dma_start(temp[:], temper)
        make_identity(nc, ident[:])
        nc.gpsimd.dma_start(gain[:], og)
        nc.sync.dma_start(slots[:], offs)
        nc.sync.dma_start(tw[:].bitcast(I32), tab_words[0].bitcast(I32))
        nc.sync.dma_start(w_raw[:], w1.rearrange("(p j) r -> p (j r)", j=4))
        nc.sync.dma_start(picks[:], offs2)
        load_scales(ts, tab_scales)
        load_scales(ds, dtab_scales)

        w_bf = t("w_bf", 4 * R, BF16)
        nc.scalar.activation(w_bf[:].rearrange("p (r j) -> p r j", j=4), w_raw[:].rearrange("p (j r) -> p r j", j=4), ACT.Copy)

        halves = [slice(h * HALF, (h + 1) * HALF) for h in range(2)]
        lists = [slots[:, h * HALF // 16 : (h + 1) * HALF // 16] for h in range(2)]

        gtw = t("gtw", J, U16)
        gts = t("gts", J, U8)
        gdw = t("gdw", J, U16)
        gds = t("gds", J, U8)
        wq = t("wq", R, U32)
        wqs = t("wqs", R, U8)
        p1 = t("p1", J, F32)
        xp1 = t("xp1", J, F32)
        nc.vector.tensor_copy(gtw[:], tw[:].indirect(slots[:]))
        dw = t("dw", T, U16, tag="tw")
        nc.sync.dma_start(dw[:].bitcast(I32), dtab_words[0].bitcast(I32))
        nc.vector.tensor_copy(gts[:, halves[0]], ts[:].indirect(lists[0]))
        nc.vector.quantize_mx(out=wq[:].bitcast(FP8X4), scales=wqs[:], in_=w_bf[:])
        nc.vector.tensor_copy(gts[:, halves[1]], ts[:].indirect(lists[1]))

        def product(name, words, scales):
            bank = ps.tile([P, HALF], F32, name=name)
            nc.tensor.matmul_mx(out=bank[:], lhsT=wq[:].bitcast(FP8X4), lhsT_scale=wqs[:], rhs=words.bitcast(FP4X4), rhs_scale=scales, start=True, stop=True)
            return bank

        for h in range(2):
            a_ps = product("a_ps%d" % h, gtw[:, halves[h]], gts[:, halves[h]])
            nc.scalar.activation(p1[:, halves[h]], a_ps[:], ACT.Exp, scale=temp[:])

        pw_ps = ps.tile([P, 2, P], F32, name="pw_ps")
        for c in range(2):
            nc.tensor.transpose(pw_ps[:, c, :], pw_cols[:, c : c + 1].to_broadcast([P, P]), ident[:])
        nc.scalar.activation(weight[:].rearrange("p (n c) -> p n c", c=2), pw_ps[:].rearrange("p c n -> p n c"), ACT.Copy)

        nc.vector.tensor_copy(gds[:], ds[:].indirect(slots[:]))
        base_sb = t("base_sb", M, F32, tag="ds")
        nc.sync.dma_start(base_sb[:], base)

        def grouped(ap):
            return ap.rearrange("p (g i) -> p g i", i=GS)

        def spread(ap):
            return ap.unsqueeze(2).to_broadcast([P, G, GS])

        s = t("s", M, F32)
        nc.vector.tensor_tensor(s[:], p1[:].indirect(picks[:]), weight[:], ALU.mult)
        dz = t("dz", M + G, F32)
        nc.vector.tensor_reduce(dz[:, M:], grouped(s[:]), AX.X, ALU.add)
        nc.vector.tensor_copy(gdw[:, halves[0]], dw[:].indirect(lists[0]))
        nc.vector.scalar_tensor_tensor(grouped(dz[:, :M]), spread(dz[:, M:]), 0.125, grouped(s[:]), ALU.mult, ALU.add)
        nc.vector.tensor_copy(gdw[:, halves[1]], dw[:].indirect(lists[1]))

        rs = t("rs", M + G, F32)
        sg = t("sg", M + G, F32)
        sq = t("sq", M + G, F32)
        nc.scalar.activation(rs[:], dz[:], ACT.Abs_reciprocal_sqrt)
        nc.scalar.activation(sg[:], dz[:], ACT.Sign)
        nc.scalar.activation(sq[:], rs[:], ACT.Square)
        rec = t("rec", M + G, F32)
        nc.vector.tensor_tensor(rec[:], sq[:], sg[:], ALU.mult)

        for h in range(2):
            ta_ps = product("ta_ps%d" % h, gdw[:, halves[h]], gds[:, halves[h]])
            nc.vector.scalar_tensor_tensor(xp1[:, halves[h]], ta_ps[:], temp[:], p1[:, halves[h]], ALU.mult, ALU.mult)

        d1 = t("d1", M, F32)
        nc.vector.scalar_tensor_tensor(d1[:], s[:], gain[:], rec[:, :M], ALU.mult, ALU.mult)
        xs = t("xs", M, F32)
        nc.vector.tensor_tensor(xs[:], xp1[:].indirect(picks[:]), weight[:], ALU.mult)
        xz = t("xz", G, F32)
        nc.vector.tensor_reduce(xz[:], grouped(xs[:]), AX.X, ALU.add)
        q = t("q", G, F32)
        e1 = t("e1", M, F32)
        e2 = t("e2", M, F32)
        f1 = t("f1", M, F32)
        res = t("res", M, F32)
        nc.vector.scalar_tensor_tensor(e1[:], xs[:], gain[:], rec[:, :M], ALU.mult, ALU.mult)
        nc.vector.tensor_tensor(q[:], xz[:], rec[:, M:], ALU.mult)
        nc.vector.tensor_tensor(e2[:], e1[:], base_sb[:], ALU.add)
        nc.vector.tensor_tensor(grouped(f1[:]), grouped(d1[:]), spread(q[:]), ALU.mult)
        nc.vector.tensor_tensor(res[:], e2[:], f1[:], ALU.subtract)
        nc.sync.dma_start(out, res[:])
